import numpy as np
import ml_dtypes


def mxq(x, axis, fmt="e4m3"):
    dtype, down = {"e4m3": (ml_dtypes.float8_e4m3fn, 7), "e5m2": (ml_dtypes.float8_e5m2, 14)}[fmt]
    v = np.moveaxis(np.asarray(x, np.float32).astype(ml_dtypes.bfloat16).astype(np.float64), axis, -1)
    blocks = v.reshape(v.shape[:-1] + (-1, 32))
    amax = np.abs(blocks).max(-1, keepdims=True)
    byte = np.maximum(np.where(amax > 0, np.frexp(amax)[1] - 1 + 127, 0) - down, 1)
    scale = np.exp2(byte - 127.0)
    codes = (blocks / scale).astype(np.float32).astype(dtype).astype(np.float64)
    return np.moveaxis((codes * scale).reshape(v.shape), -1, axis)


WIDE = False


def mx_kscale(k):
    if not WIDE:
        return np.ones(k)
    levels = np.array([10, -10, 5, -5, 0])
    if k % 512:
        return np.exp2(np.random.permutation(np.resize(levels, k // 32))).repeat(32)
    a = np.empty((k // 512, 16))
    for p in range(k // 512):
        a[p, :8] = np.random.permutation(np.resize(levels, 8))
        for g in range(8):
            far = levels[np.abs(levels - a[p, g]) >= 10]
            a[p, g + 8] = far[np.random.randint(len(far))]
    return np.exp2(a.ravel()).repeat(32)


def f64(x):
    return np.asarray(x).astype(np.float64)


def striped8(idx):
    return np.asarray(idx).reshape(8, -1, 16).transpose(0, 2, 1).reshape(128, -1).astype(np.uint16)


def unstriped8(offs):
    return offs.reshape(8, 16, -1).transpose(0, 2, 1).reshape(8, -1).astype(np.int64)


def pick8(x, idx, run):
    r = np.arange(len(x))
    return x[r[:, None], idx[r % (8 * run) // run]]


E2M1 = np.array([0.0, 0.5, 1.0, 1.5, 2.0, 3.0, 4.0, 6.0, -0.0, -0.5, -1.0, -1.5, -2.0, -3.0, -4.0, -6.0])


def pack_weight(w, fmt):
    k, n = w.shape
    w = f64(np.asarray(w, np.float32).astype(ml_dtypes.bfloat16)).reshape(k // 32, 32, n)
    amax = np.abs(w).max(1)
    if fmt == "e4m3":
        byte = np.frexp(amax)[1] - 1 + 127 - 7
    else:
        mant, ex = np.frexp(amax / 6.0)
        byte = np.where(mant > 0.5, ex, ex - 1) + 127
    byte = np.clip(np.where(amax > 0, byte, 1), 1, 254)
    scaled = (w * np.exp2(127.0 - byte)[:, None, :]).reshape(k, n).astype(np.float32)
    by_word = np.ascontiguousarray(scaled.reshape(k // 512, 128, 4, n).transpose(0, 1, 3, 2))
    if fmt == "e4m3":
        words = by_word.astype(ml_dtypes.float8_e4m3fn).view(np.uint8)
    else:
        c = by_word.astype(ml_dtypes.float4_e2m1fn).view(np.uint8) & 0xF
        words = (c[..., 0::2] | (c[..., 1::2] << 4)).reshape(k // 512, 128, 2 * n)
    return np.ascontiguousarray(words), np.ascontiguousarray(byte.astype(np.uint8).reshape(k // 512, 16, n))


def unpack_weight(words, scales, fmt):
    g, _, n = scales.shape
    words = np.ascontiguousarray(words).reshape(g, 128, n, -1)
    if fmt == "e4m3":
        vals = words.view(ml_dtypes.float8_e4m3fn).astype(np.float64)
    else:
        nib = np.empty((g, 128, n, 4), np.uint8)
        nib[..., 0::2] = words & 0xF
        nib[..., 1::2] = words >> 4
        vals = E2M1[nib]
    vals = vals * np.repeat(np.exp2(scales.astype(np.float64) - 127.0), 8, axis=1)[..., None]
    return vals.transpose(0, 1, 3, 2).reshape(g * 512, n)


D, T, I, Q = 512, 1024, 512, 128


def setup_inputs():
    n = np.random.standard_normal
    idx = np.stack([np.random.permutation(T)[:I] for _ in range(8)])
    idx2 = np.stack([np.random.permutation(T)[:I] for _ in range(8)])
    idx3 = np.stack([np.random.permutation(T)[:I] for _ in range(8)])
    idx4 = np.stack([np.random.permutation(T)[:I] for _ in range(8)])
    idx5 = np.stack([np.random.permutation(T)[:I] for _ in range(8)])
    fd = mx_kscale(D)
    keysp = pack_weight(n((D, T)) / fd[:, None], "e4m3")
    tagsp = pack_weight(n((D, T)) / fd[:, None], "e2m1")
    return {
        "query": (n((D, Q)) * 0.75 / np.sqrt(D) * fd[:, None]).astype(np.float32),
        "query2": (n((D, Q)) * 0.75 / np.sqrt(D) * fd[:, None]).astype(np.float32),
        "keys_words": keysp[0],
        "keys_scales": keysp[1],
        "tags_words": tagsp[0],
        "tags_scales": tagsp[1],
        "lam": (np.random.uniform(0.4, 1.2, (Q, 1))).astype(np.float32),
        "offs": striped8(idx),
        "offs2": striped8(idx2),
        "offs3": striped8(idx3),
        "offs4": striped8(idx4),
        "offs5": striped8(idx5),
    }


def reference(query, query2, keys_words, keys_scales, tags_words, tags_scales, lam, offs, offs2, offs3, offs4, offs5):
    idx = unstriped8(offs)
    idx2 = unstriped8(offs2)
    idx3 = unstriped8(offs3)
    idx4 = unstriped8(offs4)
    idx5 = unstriped8(offs5)
    keysu = unpack_weight(keys_words, keys_scales, "e4m3")
    tagsu = unpack_weight(tags_words, tags_scales, "e2m1")
    queryq = mxq(f64(query), 0, "e4m3")
    query2q = mxq(f64(query2), 0, "e4m3")
    a = queryq.T @ keysu + query2q.T @ tagsu
    f1 = np.zeros((Q, T))
    f1[np.arange(Q)[:, None], idx2[np.arange(Q) % 128 // 16]] = pick8(a, idx, 16)
    c1 = a + f1
    f2 = np.zeros((Q, T))
    f2[np.arange(Q)[:, None], idx4[np.arange(Q) % 128 // 16]] = pick8(c1, idx3, 16)
    c2 = c1 + f2 * f64(lam)
    y = pick8(c2, idx5, 16)
    return y

@@ -1,0 +1,122 @@
+from contextlib import ExitStack
+
+import concourse.mybir as mybir
+
+D, T, SLOTS, Q = 512, 1024, 512, 128
+FLOPS = 2 * 2 * D * Q * T
+
+F32 = mybir.dt.float32
+BF16 = mybir.dt.bfloat16
+I32 = mybir.dt.int32
+U32 = mybir.dt.uint32
+U16 = mybir.dt.uint16
+U8 = mybir.dt.uint8
+FP8X4 = mybir.dt.float8_e4m3fn_x4
+FP4X4 = mybir.dt.float4_e2m1fn_x4
+ADD = mybir.AluOpType.add
+MULT = mybir.AluOpType.mult
+COPY = mybir.ActivationFunctionType.Copy
+
+P = 128
+PACK = 4
+HALF = T // 2
+BANK = 256
+LIST_COLS = SLOTS // 16
+
+
+def tile_attend_hops_parts_kernel(tc, query, query2, keys_words, keys_scales, tags_words, tags_scales, lam,
+                                   offs, offs2, offs3, offs4, offs5, out):
+    nc = tc.nc
+    with ExitStack() as ctx:
+        sb = ctx.enter_context(tc.tile_pool(name="sb", bufs=1))
+        psum = ctx.enter_context(tc.psum_pool(name="psum", bufs=1))
+
+        tag_scale = sb.tile([P, T], U8, name="tag_scale", align_bytes=64)
+        key_scale = sb.tile([P, T], U8, name="key_scale", align_bytes=64)
+        for plane, src in ((tag_scale, tags_scales), (key_scale, keys_scales)):
+            for quad in range(4):
+                nc.scalar.dma_start(out=plane[32 * quad : 32 * quad + 4, :].bitcast(I32),
+                                    in_=src[0, 4 * quad : 4 * quad + 4, :].bitcast(I32))
+
+        def load_query(src, name):
+            raw = sb.tile([P, PACK, Q], F32, name=name)
+            nc.sync.dma_start(out=raw[:], in_=src.rearrange("(p j) w -> p j w", j=PACK))
+            return raw
+
+        def load_words(src, half, nbytes, name):
+            words = sb.tile([P, HALF * nbytes], U8, name=name, align_bytes=64)
+            nc.sync.dma_start(out=words[:].bitcast(I32),
+                              in_=src[:, half * HALF * nbytes : (half + 1) * HALF * nbytes].bitcast(I32))
+            return words
+
+        key_bytes = keys_words[0].rearrange("p n t -> p (n t)")
+        tag_bytes = tags_words[0]
+        raw2 = load_query(query2, "raw2")
+        tags0 = load_words(tag_bytes, 0, 2, "tags0")
+        raw1 = load_query(query, "raw1")
+        tags1 = load_words(tag_bytes, 1, 2, "tags1")
+        keys0 = load_words(key_bytes, 0, 4, "keys0")
+        keys1 = load_words(key_bytes, 1, 4, "keys1")
+        lists = []
+        for k, src in enumerate((offs, offs2, offs3, offs4, offs5)):
+            held = sb.tile([P, LIST_COLS], U16, name="list%d" % k)
+            nc.sync.dma_start(held[:], src)
+            lists.append(held)
+        lam_col = sb.tile([P, 1], F32, name="lam_col")
+        nc.sync.dma_start(out=lam_col[:], in_=lam)
+
+        f1 = sb.tile([P, T], F32, name="f1")
+        f2 = sb.tile([P, T], F32, name="f2")
+        nc.vector.memset(f1[:], 0.0)
+        nc.vector.memset(f2[:], 0.0)
+
+        def quantise(raw, name):
+            grouped = sb.tile([P, Q, PACK], BF16, name=name + "_bf", align_bytes=64)
+            nc.vector.tensor_copy(out=grouped[:], in_=raw[:].rearrange("p j w -> p w j"))
+            codes = sb.tile([P, Q], U32, name=name + "_codes", align_bytes=64)
+            scale = sb.tile([P, Q], U8, name=name + "_scale", align_bytes=64)
+            nc.vector.quantize_mx(out=codes[:].bitcast(FP8X4), scales=scale[:],
+                                  in_=grouped[:].rearrange("p w j -> p (w j)"))
+            return codes, scale
+
+        q2_codes, q2_scale = quantise(raw2, "q2")
+        q1_codes, q1_scale = quantise(raw1, "q1")
+
+        banks = [psum.tile([P, BANK], F32, name="bank%d" % b) for b in range(T // BANK)]
+        per_half = HALF // BANK
+        for b, bank in enumerate(banks):
+            c0 = (b % per_half) * BANK
+            nc.tensor.matmul_mx(out=bank[:], lhsT=q2_codes[:].bitcast(FP8X4), lhsT_scale=q2_scale[:],
+                                rhs=(tags0, tags1)[b // per_half][:, 2 * c0 : 2 * (c0 + BANK)].bitcast(FP4X4),
+                                rhs_scale=tag_scale[:, b * BANK : (b + 1) * BANK], start=True, stop=False)
+        a = sb.tile([P, T], F32, name="a")
+        for b, bank in enumerate(banks):
+            c0 = (b % per_half) * BANK
+            nc.tensor.matmul_mx(out=bank[:], lhsT=q1_codes[:].bitcast(FP8X4), lhsT_scale=q1_scale[:],
+                                rhs=(keys0, keys1)[b // per_half][:, 4 * c0 : 4 * (c0 + BANK)].bitcast(FP8X4),
+                                rhs_scale=key_scale[:, b * BANK : (b + 1) * BANK], start=False, stop=True)
+            if b % 2 == 0:
+                nc.scalar.activation(a[:, b * BANK : (b + 1) * BANK], bank[:], COPY)
+            else:
+                nc.vector.tensor_copy(a[:, b * BANK : (b + 1) * BANK], bank[:])
+
+        def gather(window, held, name):
+            picked = sb.tile([P, SLOTS], F32, name=name)
+            mid = LIST_COLS // 2
+            nc.vector.tensor_copy(picked[:, : SLOTS // 2], window[:].indirect(held[:, :mid]))
+            nc.scalar.activation(picked[:, SLOTS // 2 :], window[:].indirect(held[:, mid:]), COPY)
+            return picked
+
+        g1 = gather(a, lists[0], "g1")
+        nc.vector.tensor_copy(f1[:].indirect(lists[1][:]), g1[:])
+        c1 = sb.tile([P, T], F32, name="c1")
+        nc.vector.tensor_tensor(c1[:], a[:], f1[:], ADD)
+
+        g2 = gather(c1, lists[2], "g2")
+        nc.vector.tensor_copy(f2[:].indirect(lists[3][:]), g2[:])
+        c2 = sb.tile([P, T], F32, name="c2")
+        nc.vector.scalar_tensor_tensor(c2[:], f2[:], lam_col[:], c1[:], MULT, ADD)
+
+        y = gather(c2, lists[4], "y")
+        nc.sync.dma_start(out=out[:, : SLOTS // 2], in_=y[:, : SLOTS // 2])
+        nc.scalar.dma_start(out=out[:, SLOTS // 2 :], in_=y[:, SLOTS // 2 :])

@@ -19,8 +19,9 @@ COPY = mybir.ActivationFunctionType.Copy
 
 P = 128
 PACK = 4
-HALF = T // 2
+EARLY = 768
 BANK = 256
+WIDTHS = (256, 256, 256, 256)
 LIST_COLS = SLOTS // 16
 
 
@@ -31,32 +32,32 @@ def tile_attend_hops_parts_kernel(tc, query, query2, keys_words, keys_scales, ta
         sb = ctx.enter_context(tc.tile_pool(name="sb", bufs=1))
         psum = ctx.enter_context(tc.psum_pool(name="psum", bufs=1))
 
-        tag_scale = sb.tile([P, T], U8, name="tag_scale", align_bytes=64)
-        key_scale = sb.tile([P, T], U8, name="key_scale", align_bytes=64)
-        for plane, src in ((tag_scale, tags_scales), (key_scale, keys_scales)):
-            for quad in range(4):
-                nc.scalar.dma_start(out=plane[32 * quad : 32 * quad + 4, :].bitcast(I32),
-                                    in_=src[0, 4 * quad : 4 * quad + 4, :].bitcast(I32))
+        def load_scales(src, name, queues):
+            plane = sb.tile([P, T], U8, name=name, align_bytes=64)
+            for quad, queue in enumerate(queues):
+                queue.dma_start(out=plane[32 * quad : 32 * quad + 4, :].bitcast(I32),
+                                in_=src[0, 4 * quad : 4 * quad + 4, :].bitcast(I32))
+            return plane
 
         def load_query(src, name):
             raw = sb.tile([P, PACK, Q], F32, name=name)
             nc.sync.dma_start(out=raw[:], in_=src.rearrange("(p j) w -> p j w", j=PACK))
             return raw
 
-        def load_words(src, half, nbytes, name):
-            words = sb.tile([P, HALF * nbytes], U8, name=name, align_bytes=64)
-            nc.sync.dma_start(out=words[:].bitcast(I32),
-                              in_=src[:, half * HALF * nbytes : (half + 1) * HALF * nbytes].bitcast(I32))
+        def load_words(src, name):
+            words = sb.tile([P, src.shape[1]], U8, name=name, align_bytes=64)
+            nc.sync.dma_start(out=words[:].bitcast(I32), in_=src.bitcast(I32))
             return words
 
         key_bytes = keys_words[0].rearrange("p n t -> p (n t)")
-        tag_bytes = tags_words[0]
         raw2 = load_query(query2, "raw2")
-        tags0 = load_words(tag_bytes, 0, 2, "tags0")
+        tag_scale = load_scales(tags_scales, "tag_scale", (nc.scalar, nc.sync, nc.scalar, nc.sync))
+        tags = load_words(tags_words[0], "tags")
         raw1 = load_query(query, "raw1")
-        tags1 = load_words(tag_bytes, 1, 2, "tags1")
-        keys0 = load_words(key_bytes, 0, 4, "keys0")
-        keys1 = load_words(key_bytes, 1, 4, "keys1")
+        keys0 = load_words(key_bytes[:, : 4 * 2 * BANK], "keys0")
+        key_scale = load_scales(keys_scales, "key_scale", (nc.sync,) * 4)
+        keys1 = load_words(key_bytes[:, 4 * 2 * BANK :], "keys1")
+        key_cols = (keys0[:, : 4 * BANK], keys0[:, 4 * BANK :], keys1[:, : 4 * BANK], keys1[:, 4 * BANK :])
         lists = []
         for k, src in enumerate((offs, offs2, offs3, offs4, offs5)):
             held = sb.tile([P, LIST_COLS], U16, name="list%d" % k)
@@ -71,8 +72,10 @@ def tile_attend_hops_parts_kernel(tc, query, query2, keys_words, keys_scales, ta
         nc.vector.memset(f2[:], 0.0)
 
         def quantise(raw, name):
-            grouped = sb.tile([P, Q, PACK], BF16, name=name + "_bf", align_bytes=64)
-            nc.vector.tensor_copy(out=grouped[:], in_=raw[:].rearrange("p j w -> p w j"))
+            grouped = sb.tile([P, Q, PACK], BF16, name="grouped", align_bytes=64)
+            turned = raw[:].rearrange("p j w -> p w j")
+            nc.vector.tensor_copy(out=grouped[:, : Q // 2, :], in_=turned[:, : Q // 2, :])
+            nc.scalar.activation(grouped[:, Q // 2 :, :], turned[:, Q // 2 :, :], COPY)
             codes = sb.tile([P, Q], U32, name=name + "_codes", align_bytes=64)
             scale = sb.tile([P, Q], U8, name=name + "_scale", align_bytes=64)
             nc.vector.quantize_mx(out=codes[:].bitcast(FP8X4), scales=scale[:],
@@ -82,23 +85,21 @@ def tile_attend_hops_parts_kernel(tc, query, query2, keys_words, keys_scales, ta
         q2_codes, q2_scale = quantise(raw2, "q2")
         q1_codes, q1_scale = quantise(raw1, "q1")
 
-        banks = [psum.tile([P, BANK], F32, name="bank%d" % b) for b in range(T // BANK)]
-        per_half = HALF // BANK
-        for b, bank in enumerate(banks):
-            c0 = (b % per_half) * BANK
+        starts = [sum(WIDTHS[:b]) for b in range(len(WIDTHS))]
+        banks = [psum.tile([P, w], F32, name="bank%d" % b) for b, w in enumerate(WIDTHS)]
+        for bank, t0, w in zip(banks, starts, WIDTHS):
             nc.tensor.matmul_mx(out=bank[:], lhsT=q2_codes[:].bitcast(FP8X4), lhsT_scale=q2_scale[:],
-                                rhs=(tags0, tags1)[b // per_half][:, 2 * c0 : 2 * (c0 + BANK)].bitcast(FP4X4),
-                                rhs_scale=tag_scale[:, b * BANK : (b + 1) * BANK], start=True, stop=False)
+                                rhs=tags[:, 2 * t0 : 2 * (t0 + w)].bitcast(FP4X4),
+                                rhs_scale=tag_scale[:, t0 : t0 + w], start=True, stop=False)
         a = sb.tile([P, T], F32, name="a")
-        for b, bank in enumerate(banks):
-            c0 = (b % per_half) * BANK
+        for b, (bank, t0, w) in enumerate(zip(banks, starts, WIDTHS)):
             nc.tensor.matmul_mx(out=bank[:], lhsT=q1_codes[:].bitcast(FP8X4), lhsT_scale=q1_scale[:],
-                                rhs=(keys0, keys1)[b // per_half][:, 4 * c0 : 4 * (c0 + BANK)].bitcast(FP8X4),
-                                rhs_scale=key_scale[:, b * BANK : (b + 1) * BANK], start=False, stop=True)
+                                rhs=key_cols[b].bitcast(FP8X4),
+                                rhs_scale=key_scale[:, t0 : t0 + w], start=False, stop=True)
             if b % 2 == 0:
-                nc.scalar.activation(a[:, b * BANK : (b + 1) * BANK], bank[:], COPY)
+                nc.scalar.activation(a[:, t0 : t0 + w], bank[:], COPY)
             else:
-                nc.vector.tensor_copy(a[:, b * BANK : (b + 1) * BANK], bank[:])
+                nc.vector.tensor_copy(a[:, t0 : t0 + w], bank[:])
 
         def gather(window, held, name):
             picked = sb.tile([P, SLOTS], F32, name=name)
@@ -110,7 +111,10 @@ def tile_attend_hops_parts_kernel(tc, query, query2, keys_words, keys_scales, ta
         g1 = gather(a, lists[0], "g1")
         nc.vector.tensor_copy(f1[:].indirect(lists[1][:]), g1[:])
         c1 = sb.tile([P, T], F32, name="c1")
-        nc.vector.tensor_tensor(c1[:], a[:], f1[:], ADD)
+        for bank, t0, w in zip(banks, starts, WIDTHS):
+            if t0 < EARLY:
+                nc.vector.tensor_tensor(c1[:, t0 : t0 + w], bank[:], f1[:, t0 : t0 + w], ADD)
+        nc.gpsimd.tensor_tensor(c1[:, EARLY:], a[:, EARLY:], f1[:, EARLY:], ADD)
 
         g2 = gather(c1, lists[2], "g2")
         nc.vector.tensor_copy(f2[:].indirect(lists[3][:]), g2[:])

from contextlib import ExitStack

import concourse.mybir as mybir

D, T, SLOTS, Q = 512, 1024, 512, 128
FLOPS = 2 * 2 * D * Q * T

F32 = mybir.dt.float32
BF16 = mybir.dt.bfloat16
I32 = mybir.dt.int32
U32 = mybir.dt.uint32
U16 = mybir.dt.uint16
U8 = mybir.dt.uint8
FP8X4 = mybir.dt.float8_e4m3fn_x4
FP4X4 = mybir.dt.float4_e2m1fn_x4
ADD = mybir.AluOpType.add
MULT = mybir.AluOpType.mult
COPY = mybir.ActivationFunctionType.Copy

P = 128
PACK = 4
EARLY = 768
BANK = 256
WIDTHS = (256, 256, 256, 256)
LIST_COLS = SLOTS // 16


def tile_attend_hops_parts_kernel(tc, query, query2, keys_words, keys_scales, tags_words, tags_scales, lam,
                                   offs, offs2, offs3, offs4, offs5, out):
    nc = tc.nc
    with ExitStack() as ctx:
        sb = ctx.enter_context(tc.tile_pool(name="sb", bufs=1))
        psum = ctx.enter_context(tc.psum_pool(name="psum", bufs=1))

        def load_scales(src, name, queues):
            plane = sb.tile([P, T], U8, name=name, align_bytes=64)
            for quad, queue in enumerate(queues):
                queue.dma_start(out=plane[32 * quad : 32 * quad + 4, :].bitcast(I32),
                                in_=src[0, 4 * quad : 4 * quad + 4, :].bitcast(I32))
            return plane

        def load_query(src, name):
            raw = sb.tile([P, PACK, Q], F32, name=name)
            nc.sync.dma_start(out=raw[:], in_=src.rearrange("(p j) w -> p j w", j=PACK))
            return raw

        def load_words(src, name):
            words = sb.tile([P, src.shape[1]], U8, name=name, align_bytes=64)
            nc.sync.dma_start(out=words[:].bitcast(I32), in_=src.bitcast(I32))
            return words

        key_bytes = keys_words[0].rearrange("p n t -> p (n t)")
        raw2 = load_query(query2, "raw2")
        tag_scale = load_scales(tags_scales, "tag_scale", (nc.scalar, nc.sync, nc.scalar, nc.sync))
        tags = load_words(tags_words[0], "tags")
        raw1 = load_query(query, "raw1")
        keys0 = load_words(key_bytes[:, : 4 * 2 * BANK], "keys0")
        key_scale = load_scales(keys_scales, "key_scale", (nc.sync,) * 4)
        keys1 = load_words(key_bytes[:, 4 * 2 * BANK :], "keys1")
        key_cols = (keys0[:, : 4 * BANK], keys0[:, 4 * BANK :], keys1[:, : 4 * BANK], keys1[:, 4 * BANK :])
        lists = []
        for k, src in enumerate((offs, offs2, offs3, offs4, offs5)):
            held = sb.tile([P, LIST_COLS], U16, name="list%d" % k)
            nc.sync.dma_start(held[:], src)
            lists.append(held)
        lam_col = sb.tile([P, 1], F32, name="lam_col")
        nc.sync.dma_start(out=lam_col[:], in_=lam)

        f1 = sb.tile([P, T], F32, name="f1")
        f2 = sb.tile([P, T], F32, name="f2")
        nc.vector.memset(f1[:], 0.0)
        nc.vector.memset(f2[:], 0.0)

        def quantise(raw, name):
            grouped = sb.tile([P, Q, PACK], BF16, name="grouped", align_bytes=64)
            turned = raw[:].rearrange("p j w -> p w j")
            nc.vector.tensor_copy(out=grouped[:, : Q // 2, :], in_=turned[:, : Q // 2, :])
            nc.scalar.activation(grouped[:, Q // 2 :, :], turned[:, Q // 2 :, :], COPY)
            codes = sb.tile([P, Q], U32, name=name + "_codes", align_bytes=64)
            scale = sb.tile([P, Q], U8, name=name + "_scale", align_bytes=64)
            nc.vector.quantize_mx(out=codes[:].bitcast(FP8X4), scales=scale[:],
                                  in_=grouped[:].rearrange("p w j -> p (w j)"))
            return codes, scale

        q2_codes, q2_scale = quantise(raw2, "q2")
        q1_codes, q1_scale = quantise(raw1, "q1")

        starts = [sum(WIDTHS[:b]) for b in range(len(WIDTHS))]
        banks = [psum.tile([P, w], F32, name="bank%d" % b) for b, w in enumerate(WIDTHS)]
        for bank, t0, w in zip(banks, starts, WIDTHS):
            nc.tensor.matmul_mx(out=bank[:], lhsT=q2_codes[:].bitcast(FP8X4), lhsT_scale=q2_scale[:],
                                rhs=tags[:, 2 * t0 : 2 * (t0 + w)].bitcast(FP4X4),
                                rhs_scale=tag_scale[:, t0 : t0 + w], start=True, stop=False)
        a = sb.tile([P, T], F32, name="a")
        for b, (bank, t0, w) in enumerate(zip(banks, starts, WIDTHS)):
            nc.tensor.matmul_mx(out=bank[:], lhsT=q1_codes[:].bitcast(FP8X4), lhsT_scale=q1_scale[:],
                                rhs=key_cols[b].bitcast(FP8X4),
                                rhs_scale=key_scale[:, t0 : t0 + w], start=False, stop=True)
            if b % 2 == 0:
                nc.scalar.activation(a[:, t0 : t0 + w], bank[:], COPY)
            else:
                nc.vector.tensor_copy(a[:, t0 : t0 + w], bank[:])

        def gather(window, held, name):
            picked = sb.tile([P, SLOTS], F32, name=name)
            mid = LIST_COLS // 2
            nc.vector.tensor_copy(picked[:, : SLOTS // 2], window[:].indirect(held[:, :mid]))
            nc.scalar.activation(picked[:, SLOTS // 2 :], window[:].indirect(held[:, mid:]), COPY)
            return picked

        g1 = gather(a, lists[0], "g1")
        nc.vector.tensor_copy(f1[:].indirect(lists[1][:]), g1[:])
        c1 = sb.tile([P, T], F32, name="c1")
        for bank, t0, w in zip(banks, starts, WIDTHS):
            if t0 < EARLY:
                nc.vector.tensor_tensor(c1[:, t0 : t0 + w], bank[:], f1[:, t0 : t0 + w], ADD)
        nc.gpsimd.tensor_tensor(c1[:, EARLY:], a[:, EARLY:], f1[:, EARLY:], ADD)

        g2 = gather(c1, lists[2], "g2")
        nc.vector.tensor_copy(f2[:].indirect(lists[3][:]), g2[:])
        c2 = sb.tile([P, T], F32, name="c2")
        nc.vector.scalar_tensor_tensor(c2[:], f2[:], lam_col[:], c1[:], MULT, ADD)

        y = gather(c2, lists[4], "y")
        nc.sync.dma_start(out=out[:, : SLOTS // 2], in_=y[:, : SLOTS // 2])
        nc.scalar.dma_start(out=out[:, SLOTS // 2 :], in_=y[:, SLOTS // 2 :])
